import numpy as np
import ml_dtypes


def mxq(x, axis, fmt="e4m3"):
    dtype, down = {"e4m3": (ml_dtypes.float8_e4m3fn, 7), "e5m2": (ml_dtypes.float8_e5m2, 14)}[fmt]
    v = np.moveaxis(np.asarray(x, np.float32).astype(ml_dtypes.bfloat16).astype(np.float64), axis, -1)
    blocks = v.reshape(v.shape[:-1] + (-1, 32))
    amax = np.abs(blocks).max(-1, keepdims=True)
    byte = np.maximum(np.where(amax > 0, np.frexp(amax)[1] - 1 + 127, 0) - down, 1)
    scale = np.exp2(byte - 127.0)
    codes = (blocks / scale).astype(np.float32).astype(dtype).astype(np.float64)
    return np.moveaxis((codes * scale).reshape(v.shape), -1, axis)


WIDE = False


def mx_kscale(k):
    if not WIDE:
        return np.ones(k)
    levels = np.array([30, -30])
    if k % 512:
        return np.exp2(np.random.permutation(np.resize(levels, k // 32))).repeat(32)
    a = np.empty((k // 512, 16))
    for p in range(k // 512):
        a[p, :8] = np.random.permutation(np.resize(levels, 8))
        for g in range(8):
            far = levels[np.abs(levels - a[p, g]) >= 10]
            a[p, g + 8] = far[np.random.randint(len(far))]
    return np.exp2(a.ravel()).repeat(32)


BF16 = ml_dtypes.bfloat16


def bf(x):
    return np.asarray(x, np.float32).astype(BF16)


def f64(x):
    return np.asarray(x).astype(np.float64)


E2M1 = np.array([0.0, 0.5, 1.0, 1.5, 2.0, 3.0, 4.0, 6.0, -0.0, -0.5, -1.0, -1.5, -2.0, -3.0, -4.0, -6.0])


def pack_weight(w, fmt):
    k, n = w.shape
    w = f64(bf(w)).reshape(k // 32, 32, n)
    amax = np.abs(w).max(1)
    if fmt == "e4m3":
        byte = np.frexp(amax)[1] - 1 + 127 - 7
    else:
        mant, ex = np.frexp(amax / 6.0)
        byte = np.where(mant > 0.5, ex, ex - 1) + 127
    byte = np.clip(np.where(amax > 0, byte, 1), 1, 254)
    scaled = (w * np.exp2(127.0 - byte)[:, None, :]).reshape(k, n).astype(np.float32)
    by_word = np.ascontiguousarray(scaled.reshape(k // 512, 128, 4, n).transpose(0, 1, 3, 2))
    if fmt == "e4m3":
        words = by_word.astype(ml_dtypes.float8_e4m3fn).view(np.uint8)
    else:
        c = by_word.astype(ml_dtypes.float4_e2m1fn).view(np.uint8) & 0xF
        words = c[..., 0::2] | (c[..., 1::2] << 4)
    return np.ascontiguousarray(words), np.ascontiguousarray(byte.astype(np.uint8).reshape(k // 512, 16, n))


def unpack_weight(words, scales, fmt):
    g, p, n, _ = words.shape
    if fmt == "e4m3":
        vals = np.ascontiguousarray(words).view(ml_dtypes.float8_e4m3fn).astype(np.float64)
    else:
        nib = np.empty((g, p, n, 4), np.uint8)
        nib[..., 0::2] = words & 0xF
        nib[..., 1::2] = words >> 4
        vals = E2M1[nib]
    vals = vals * np.repeat(np.exp2(scales.astype(np.float64) - 127.0), 8, axis=1)[..., None]
    return vals.transpose(0, 1, 3, 2).reshape(g * 512, n)
def pack4(w):
    words, scales = pack_weight(w, "e2m1")
    return words.reshape(words.shape[0], 128, -1), scales


def unpack4(words, scales):
    return unpack_weight(words.reshape(words.shape[0], 128, -1, 2), scales, "e2m1")


M, K, N, D = 1024, 2048, 1536, 512


def setup_inputs():
    s, t = mx_kscale(K), mx_kscale(N)
    x = np.random.standard_normal((M, K)) * s
    refs = 2.0 * np.random.standard_normal((K, N)) / np.sqrt(K) / s[:, None]
    refs_words, refs_scales = pack4(refs)
    theta = 1.0 + 0.5 * np.random.standard_normal(M)
    c = (1.0 + 0.1 * np.random.standard_normal(N)) * t
    v = np.random.standard_normal((N, D)) / np.sqrt(N) / t[:, None]
    return {"x": bf(x),
            "refs_words": refs_words,
            "refs_scales": refs_scales,
            "theta": bf(theta),
            "c": bf(c),
            "v": bf(v)}


def reference(x, refs_words, refs_scales, theta, c, v):
    ident = mxq(f64(x), 1, "e4m3") @ unpack4(refs_words, refs_scales)
    near = 1.0 / (1.0 + np.exp(f64(theta)[:, None] - ident))
    count = near.mean(axis=1, keepdims=True)
    a = near * f64(c)
    profile = mxq(a, 1, "e5m2") @ mxq(f64(v), 0, "e4m3")
    return profile / count

@@ -1,0 +1,335 @@
+from contextlib import ExitStack
+
+import concourse.mybir as mybir
+from concourse.masks import make_identity
+
+M, K, N, D = 1024, 2048, 1536, 512
+FLOPS = 2 * M * N * (K + D)
+
+F32 = mybir.dt.float32
+BF16 = mybir.dt.bfloat16
+I32 = mybir.dt.int32
+U32 = mybir.dt.uint32
+U8 = mybir.dt.uint8
+E4M3 = mybir.dt.float8_e4m3fn_x4
+E5M2 = mybir.dt.float8_e5m2_x4
+E2M1 = mybir.dt.float4_e2m1fn_x4
+ACT = mybir.ActivationFunctionType
+ALU = mybir.AluOpType
+
+P = 128
+BANK = 512
+TILES = M // P
+KG = K // 512
+NG = N // 512
+LAG = 3
+
+
+def tile_msa_neighbour_reweighting_s9_kernel(tc, x, refs_words, refs_scales, theta, c, v, out):
+    nc = tc.nc
+    x_rows = x.rearrange("(p i) k -> p i k", i=TILES)
+    out_rows = out.rearrange("(p i) d -> p i d", i=TILES)
+
+    with ExitStack() as ctx:
+        keep = ctx.enter_context(tc.tile_pool(name="keep", bufs=1))
+        work = ctx.enter_context(tc.tile_pool(name="work", bufs=3))
+        psum = ctx.enter_context(tc.psum_pool(name="psum", bufs=1))
+        ctx.enter_context(tc.manual_schedule())
+
+        def bank(tag):
+            return psum.tile([P, BANK], F32, name=tag, tag=tag)
+
+        x_half = {}
+        for h in range(2):
+            first = keep.tile([P, K // 2], BF16, name="x0_%d" % h)
+            nc.sync.dma_start(out=first[:], in_=x_rows[:, 0, h * 1024 : (h + 1) * 1024])
+            x_half[0, h] = first[:]
+
+        def load_x(i):
+            whole = keep.tile([P, K], BF16, name="x%d" % i)
+            nc.sync.dma_start(out=whole[:], in_=x_rows[:, i, :])
+            for h in range(2):
+                x_half[i, h] = whole[:, h * 1024 : (h + 1) * 1024]
+
+        ident = keep.tile([P, P], F32)
+        make_identity(nc, ident[:])
+
+        w_scales = keep.tile([P, KG * N], U8, align_bytes=64)
+        nc.vector.memset(w_scales[:].bitcast(I32), 0)
+        scale_rows = refs_scales.bitcast(I32).rearrange("g (q r) n -> r q g n", r=4)
+        for r in range(4):
+            nc.sync.dma_start(
+                out=w_scales[r:P:32, :].bitcast(I32).rearrange("q (g n) -> q g n", g=KG),
+                in_=scale_rows[r],
+            )
+
+        w_codes = []
+
+        def load_w(j):
+            part = keep.tile([P, KG, 2 * BANK], U8, name="w%d" % j, align_bytes=64)
+            src = refs_words.rearrange("g p b -> p g b")[:, :, j * 2 * BANK : (j + 1) * 2 * BANK]
+            nc.sync.dma_start(out=part[:].bitcast(I32), in_=src.bitcast(I32))
+            w_codes.append(part)
+
+        v_raw = []
+
+        def load_v(g):
+            rows = keep.tile([P, 4, D], BF16, name="v%d" % g)
+            nc.sync.dma_start(out=rows[:], in_=v[g * 512 : (g + 1) * 512, :].rearrange("(p t) d -> p t d", t=4))
+            v_raw.append(rows)
+
+        load_w(0)
+        load_x(1)
+        c_cols = keep.tile([P, NG, 4], BF16)
+        nc.scalar.dma_start(out=c_cols[:], in_=c.rearrange("(g p t) -> p g t", p=P, t=4))
+        theta_sb = keep.tile([P, TILES], BF16)
+        nc.scalar.dma_start(out=theta_sb[:], in_=theta.rearrange("(p i) -> p i", i=TILES))
+        load_w(1)
+        load_w(2)
+        load_v(0)
+        load_x(2)
+        load_v(1)
+        load_x(3)
+        load_v(2)
+        for i in range(4, TILES):
+            load_x(i)
+
+        x_sorted, x_banks, x_grouped, x_codes, x_scales = {}, {}, {}, {}, {}
+        s_banks, near, parts, a_rows = {}, {}, {}, {}
+        a_banks, a_grouped, a_codes, a_scales = {}, {}, {}, {}
+        mean, inv_mean, o_banks = {}, {}, {}
+
+        def sort_x(i, h):
+            x_sorted[i, h] = work.tile([P, BANK], F32, name="x_sorted", bufs=4)
+            nc.vector.tensor_copy(
+                out=x_sorted[i, h][:].rearrange("m (u a w) -> m a u w", u=2, w=4),
+                in_=x_half[i, h].bitcast(F32).rearrange("m (a w u) -> m a u w", u=2, w=4),
+            )
+
+        def turn_x(i, h):
+            x_banks[i, h] = bank("xt%d" % h)
+            for g in range(2):
+                for u in range(2):
+                    nc.tensor.transpose(
+                        x_banks[i, h][:, (2 * g + u) * P : (2 * g + u + 1) * P],
+                        x_sorted[i, h][:, (2 * u + g) * P : (2 * u + g + 1) * P],
+                        ident[:],
+                    )
+
+        def group_words(src_bank, groups, name):
+            grouped = work.tile([P, groups * BANK], BF16, name=name, align_bytes=64)
+            nc.scalar.copy(
+                out=grouped[:].bitcast(F32).rearrange("p (g m u) -> p g m u", u=2, m=P),
+                in_=src_bank[:, : groups * 2 * P].rearrange("p (g u m) -> p g m u", u=2, m=P),
+            )
+            return grouped
+
+        def group_x(i, h):
+            x_grouped[i, h] = group_words(x_banks[i, h], 2, "x_grouped")
+
+        def quantise_x(i, h):
+            if h == 0:
+                x_codes[i] = work.tile([P, KG * P], U32, name="x_codes", align_bytes=64)
+                x_scales[i] = work.tile([P, KG * P], U8, name="x_scales", align_bytes=64)
+            cols = slice(h * 2 * P, (h + 1) * 2 * P)
+            nc.vector.quantize_mx(out=x_codes[i][:, cols].bitcast(E4M3), scales=x_scales[i][:, cols], in_=x_grouped[i, h][:])
+
+        def scores(i, j):
+            s_banks[i, j] = bank("s%d" % j)
+            for g in range(KG):
+                cols = slice(g * P, (g + 1) * P)
+                nc.tensor.matmul_mx(
+                    out=s_banks[i, j][:],
+                    lhsT=x_codes[i][:, cols].bitcast(E4M3),
+                    lhsT_scale=x_scales[i][:, cols],
+                    rhs=w_codes[j][:, g, :].bitcast(E2M1),
+                    rhs_scale=w_scales[:, g * N + j * BANK : g * N + (j + 1) * BANK],
+                    start=(g == 0),
+                    stop=(g == KG - 1),
+                )
+
+        def sigmoid(i, j):
+            if j == 0:
+                parts[i] = work.tile([P, NG], F32, name="parts")
+            near[i, j] = work.tile([P, BANK], F32, name="near")
+            nc.scalar.activation(
+                out=near[i, j][:].rearrange("m (u p e) -> m u p e", u=2, e=2),
+                in_=s_banks[i, j][:].rearrange("m (p u e) -> m u p e", u=2, e=2),
+                func=ACT.Sigmoid,
+                bias=neg_theta[:, i : i + 1],
+                accum_out=parts[i][:, j : j + 1],
+            )
+
+        def weigh(i, j):
+            a_rows[i, j] = work.tile([P, BANK], BF16, name="a_rows", bufs=6)
+            nc.vector.tensor_tensor(
+                out=a_rows[i, j][:], in0=near[i, j][:], in1=c_all[:, j * BANK : (j + 1) * BANK], op=ALU.mult
+            )
+
+        def mean_near(i):
+            shares = work.tile([P, NG], F32, name="shares")
+            mean[i] = work.tile([P, 1], F32, name="mean")
+            nc.vector.tensor_scalar(
+                out=shares[:], in0=parts[i][:], scalar1=1.0 / N, scalar2=None, op0=ALU.mult, op1=ALU.add, accum_out=mean[i][:]
+            )
+
+        def invert_mean(i):
+            inv_mean[i] = keep.tile([P, 1], F32, name="inv_mean%d" % i)
+            nc.vector.reciprocal(out=inv_mean[i][:], in_=mean[i][:])
+
+        def turn_a(i, b):
+            a_banks[i, b] = bank("at%d" % b)
+            for g in range(2 * b, min(2 * b + 2, NG)):
+                words = a_rows[i, g][:].bitcast(F32)
+                for u in range(2):
+                    at = (2 * (g - 2 * b) + u) * P
+                    nc.tensor.transpose(a_banks[i, b][:, at : at + P], words[:, u * P : (u + 1) * P], ident[:])
+
+        def group_a(i, b):
+            a_grouped[i, b] = group_words(a_banks[i, b], 2 - b, "a_grouped%d" % b)
+
+        def quantise_a(i, b):
+            if b == 0:
+                a_codes[i] = keep.tile([P, NG * P], U32, name="a_codes%d" % i, align_bytes=64)
+                a_scales[i] = keep.tile([P, NG * P], U8, name="a_scales%d" % i, align_bytes=64)
+            cols = slice(b * 2 * P, min((b + 1) * 2 * P, NG * P))
+            nc.vector.quantize_mx(out=a_codes[i][:, cols].bitcast(E5M2), scales=a_scales[i][:, cols], in_=a_grouped[i, b][:])
+
+        def profile(i, tag, groups=range(NG)):
+            if 0 in groups:
+                o_banks[i] = bank(tag)
+            for g in groups:
+                cols = slice(g * P, (g + 1) * P)
+                nc.tensor.matmul_mx(
+                    out=o_banks[i][:],
+                    lhsT=a_codes[i][:, cols].bitcast(E5M2),
+                    lhsT_scale=a_scales[i][:, cols],
+                    rhs=v_codes[:, g * D : (g + 1) * D].bitcast(E4M3),
+                    rhs_scale=v_scales[:, g * D : (g + 1) * D],
+                    start=(g == 0),
+                    stop=(g == NG - 1),
+                )
+
+        def finish(i):
+            result = work.tile([P, D], F32, name="result")
+            nc.scalar.activation(out=result[:], in_=o_banks[i][:], func=ACT.Copy, scale=inv_mean[i][:])
+            nc.sync.dma_start(out=out_rows[:, i, :], in_=result[:])
+
+        v_grouped = {}
+        v_codes = keep.tile([P, NG * D], U32, align_bytes=64)
+        v_scales = keep.tile([P, NG * D], U8, align_bytes=64)
+
+        def group_v(g, h):
+            if h == 0:
+                v_grouped[g] = keep.tile([P, D, 4], BF16, name="v_grouped%d" % g, align_bytes=64)
+            cols = slice(h * D // 2, (h + 1) * D // 2)
+            nc.vector.tensor_copy(
+                out=v_grouped[g][:, cols, :].rearrange("p (a w) t -> p a t w", w=4),
+                in_=v_raw[g][:, :, cols].rearrange("p t (a w) -> p a t w", w=4),
+            )
+
+        def quantise_v(g):
+            cols = slice(g * D, (g + 1) * D)
+            nc.vector.quantize_mx(
+                out=v_codes[:, cols].bitcast(E4M3), scales=v_scales[:, cols], in_=v_grouped[g][:].rearrange("p d t -> p (d t)")
+            )
+
+        v_steps = []
+        for g in range(NG):
+            v_steps.extend([lambda g=g: group_v(g, 0), lambda g=g: group_v(g, 1), lambda g=g: quantise_v(g)])
+
+        def some_v():
+            if v_steps:
+                v_steps[0]()
+                v_steps.remove(v_steps[0])
+
+        for h in range(2):
+            sort_x(0, h)
+            turn_x(0, h)
+            group_x(0, h)
+        c_all = keep.tile([P, N], BF16)
+        c_words = c_cols[:].rearrange("p g t -> p (g t)").bitcast(F32)
+        c_banks = [bank("at0"), bank("at1")]
+        for w in range(2 * NG):
+            nc.tensor.transpose(
+                c_banks[w // 4][:, (w % 4) * P : (w % 4 + 1) * P], c_words[:, w : w + 1].to_broadcast([P, P]), ident[:]
+            )
+        quantise_x(0, 0)
+        quantise_x(0, 1)
+        neg_theta = keep.tile([P, TILES], F32)
+        nc.vector.tensor_scalar(out=neg_theta[:], in0=theta_sb[:], scalar1=-1.0, scalar2=None, op0=ALU.mult)
+        sort_x(1, 0)
+        sort_x(1, 1)
+        nc.vector.tensor_copy(out=c_all[:, : 2 * BANK].bitcast(F32), in_=c_banks[0][:])
+        nc.vector.tensor_copy(out=c_all[:, 2 * BANK :].bitcast(F32), in_=c_banks[1][:, : 2 * P])
+
+        last = TILES - 1
+        for i in range(TILES):
+            scores(i, 0)
+            if i > LAG:
+                finish(i - LAG - 1)
+            if i > 0:
+                mean_near(i - 1)
+                some_v()
+                invert_mean(i - 1)
+            sigmoid(i, 0)
+            if i < last:
+                turn_x(i + 1, 0)
+                turn_x(i + 1, 1)
+            if i > 0:
+                turn_a(i - 1, 0)
+                turn_a(i - 1, 1)
+            weigh(i, 0)
+            if i < last:
+                group_x(i + 1, 0)
+                group_x(i + 1, 1)
+                quantise_x(i + 1, 0)
+                quantise_x(i + 1, 1)
+            if i == last:
+                profile(i - LAG, "o")
+            scores(i, 1)
+            if i > 0:
+                group_a(i - 1, 0)
+                group_a(i - 1, 1)
+            if i + 2 < TILES and i > 0:
+                sort_x(i + 2, 0)
+                sort_x(i + 2, 1)
+            if i > 0:
+                quantise_a(i - 1, 0)
+                quantise_a(i - 1, 1)
+            if i == last:
+                finish(i - LAG)
+            sigmoid(i, 1)
+            weigh(i, 1)
+            if i == last:
+                profile(i - LAG + 1, "xt0")
+            scores(i, 2)
+            some_v()
+            if i == 0:
+                some_v()
+                sort_x(2, 0)
+                sort_x(2, 1)
+            if i == 2:
+                some_v()
+            if i == last:
+                finish(i - LAG + 1)
+            sigmoid(i, 2)
+            if LAG <= i < last:
+                profile(i - LAG, "o")
+            if i < last:
+                weigh(i, 2)
+
+        turn_a(last, 0)
+        weigh(last, 2)
+        group_a(last, 0)
+        profile(last - 1, "xt1")
+        turn_a(last, 1)
+        quantise_a(last, 0)
+        mean_near(last)
+        group_a(last, 1)
+        profile(last, "o", range(2))
+        invert_mean(last)
+        quantise_a(last, 1)
+        finish(last - 1)
+        profile(last, "o", range(2, NG))
+        finish(last)

@@ -22,7 +22,7 @@ BANK = 512
 TILES = M // P
 KG = K // 512
 NG = N // 512
-LAG = 3
+FIRST = 5
 
 
 def tile_msa_neighbour_reweighting_s9_kernel(tc, x, refs_words, refs_scales, theta, c, v, out):
@@ -54,15 +54,6 @@ def tile_msa_neighbour_reweighting_s9_kernel(tc, x, refs_words, refs_scales, the
         ident = keep.tile([P, P], F32)
         make_identity(nc, ident[:])
 
-        w_scales = keep.tile([P, KG * N], U8, align_bytes=64)
-        nc.vector.memset(w_scales[:].bitcast(I32), 0)
-        scale_rows = refs_scales.bitcast(I32).rearrange("g (q r) n -> r q g n", r=4)
-        for r in range(4):
-            nc.sync.dma_start(
-                out=w_scales[r:P:32, :].bitcast(I32).rearrange("q (g n) -> q g n", g=KG),
-                in_=scale_rows[r],
-            )
-
         w_codes = []
 
         def load_w(j):
@@ -78,16 +69,33 @@ def tile_msa_neighbour_reweighting_s9_kernel(tc, x, refs_words, refs_scales, the
             nc.sync.dma_start(out=rows[:], in_=v[g * 512 : (g + 1) * 512, :].rearrange("(p t) d -> p t d", t=4))
             v_raw.append(rows)
 
+        w_scales = {}
+
+        def load_scales(thirds):
+            width = len(thirds) * BANK
+            plane = keep.tile([P, KG * width], U8, name="w_scales%d" % thirds[0], align_bytes=64)
+            nc.vector.memset(plane[:].bitcast(I32), 0)
+            cols = slice(thirds[0] * BANK, thirds[0] * BANK + width)
+            rows = refs_scales[:, :, cols].bitcast(I32).rearrange("g (q r) n -> r q g n", r=4)
+            for r in range(4):
+                nc.sync.dma_start(out=plane[r:P:32, :].bitcast(I32).rearrange("q (g n) -> q g n", g=KG), in_=rows[r])
+            for j in thirds:
+                for g in range(KG):
+                    at = g * width + (j - thirds[0]) * BANK
+                    w_scales[j, g] = plane[:, at : at + BANK]
+
+        load_scales([0])
         load_w(0)
-        load_x(1)
         c_cols = keep.tile([P, NG, 4], BF16)
         nc.scalar.dma_start(out=c_cols[:], in_=c.rearrange("(g p t) -> p g t", p=P, t=4))
         theta_sb = keep.tile([P, TILES], BF16)
         nc.scalar.dma_start(out=theta_sb[:], in_=theta.rearrange("(p i) -> p i", i=TILES))
+        load_scales([1, 2])
         load_w(1)
+        load_x(1)
         load_w(2)
-        load_v(0)
         load_x(2)
+        load_v(0)
         load_v(1)
         load_x(3)
         load_v(2)
@@ -116,8 +124,8 @@ def tile_msa_neighbour_reweighting_s9_kernel(tc, x, refs_words, refs_scales, the
                         ident[:],
                     )
 
-        def group_words(src_bank, groups, name):
-            grouped = work.tile([P, groups * BANK], BF16, name=name, align_bytes=64)
+        def group_words(src_bank, groups, name, bufs):
+            grouped = work.tile([P, groups * BANK], BF16, name=name, align_bytes=64, bufs=bufs)
             nc.scalar.copy(
                 out=grouped[:].bitcast(F32).rearrange("p (g m u) -> p g m u", u=2, m=P),
                 in_=src_bank[:, : groups * 2 * P].rearrange("p (g u m) -> p g m u", u=2, m=P),
@@ -125,7 +133,7 @@ def tile_msa_neighbour_reweighting_s9_kernel(tc, x, refs_words, refs_scales, the
             return grouped
 
         def group_x(i, h):
-            x_grouped[i, h] = group_words(x_banks[i, h], 2, "x_grouped")
+            x_grouped[i, h] = group_words(x_banks[i, h], 2, "x_grouped", 3)
 
         def quantise_x(i, h):
             if h == 0:
@@ -143,14 +151,14 @@ def tile_msa_neighbour_reweighting_s9_kernel(tc, x, refs_words, refs_scales, the
                     lhsT=x_codes[i][:, cols].bitcast(E4M3),
                     lhsT_scale=x_scales[i][:, cols],
                     rhs=w_codes[j][:, g, :].bitcast(E2M1),
-                    rhs_scale=w_scales[:, g * N + j * BANK : g * N + (j + 1) * BANK],
+                    rhs_scale=w_scales[j, g],
                     start=(g == 0),
                     stop=(g == KG - 1),
                 )
 
         def sigmoid(i, j):
             if j == 0:
-                parts[i] = work.tile([P, NG], F32, name="parts")
+                parts[i] = keep.tile([P, NG], F32, name="parts%d" % i)
             near[i, j] = work.tile([P, BANK], F32, name="near")
             nc.scalar.activation(
                 out=near[i, j][:].rearrange("m (u p e) -> m u p e", u=2, e=2),
@@ -186,7 +194,7 @@ def tile_msa_neighbour_reweighting_s9_kernel(tc, x, refs_words, refs_scales, the
                     nc.tensor.transpose(a_banks[i, b][:, at : at + P], words[:, u * P : (u + 1) * P], ident[:])
 
         def group_a(i, b):
-            a_grouped[i, b] = group_words(a_banks[i, b], 2 - b, "a_grouped%d" % b)
+            a_grouped[i, b] = group_words(a_banks[i, b], 2 - b, "a_grouped%d" % b, FIRST + 1)
 
         def quantise_a(i, b):
             if b == 0:
@@ -210,10 +218,12 @@ def tile_msa_neighbour_reweighting_s9_kernel(tc, x, refs_words, refs_scales, the
                     stop=(g == NG - 1),
                 )
 
-        def finish(i):
+        def finish(i, pieces=1):
             result = work.tile([P, D], F32, name="result")
-            nc.scalar.activation(out=result[:], in_=o_banks[i][:], func=ACT.Copy, scale=inv_mean[i][:])
-            nc.sync.dma_start(out=out_rows[:, i, :], in_=result[:])
+            for piece in range(pieces):
+                cols = slice(piece * D // pieces, (piece + 1) * D // pieces)
+                nc.scalar.activation(out=result[:, cols], in_=o_banks[i][:, cols], func=ACT.Copy, scale=inv_mean[i][:])
+                nc.sync.dma_start(out=out_rows[:, i, cols], in_=result[:, cols])
 
         v_grouped = {}
         v_codes = keep.tile([P, NG * D], U32, align_bytes=64)
@@ -249,73 +259,94 @@ def tile_msa_neighbour_reweighting_s9_kernel(tc, x, refs_words, refs_scales, the
             group_x(0, h)
         c_all = keep.tile([P, N], BF16)
         c_words = c_cols[:].rearrange("p g t -> p (g t)").bitcast(F32)
-        c_banks = [bank("at0"), bank("at1")]
-        for w in range(2 * NG):
-            nc.tensor.transpose(
-                c_banks[w // 4][:, (w % 4) * P : (w % 4 + 1) * P], c_words[:, w : w + 1].to_broadcast([P, P]), ident[:]
-            )
+
+        def spread_c():
+            c_banks = [bank("at0"), bank("at1")]
+            for w in range(2 * NG):
+                nc.tensor.transpose(
+                    c_banks[w // 4][:, (w % 4) * P : (w % 4 + 1) * P], c_words[:, w : w + 1].to_broadcast([P, P]), ident[:]
+                )
+            nc.vector.tensor_copy(out=c_all[:, : 2 * BANK].bitcast(F32), in_=c_banks[0][:])
+            nc.vector.tensor_copy(out=c_all[:, 2 * BANK :].bitcast(F32), in_=c_banks[1][:, : 2 * P])
+
         quantise_x(0, 0)
         quantise_x(0, 1)
         neg_theta = keep.tile([P, TILES], F32)
         nc.vector.tensor_scalar(out=neg_theta[:], in0=theta_sb[:], scalar1=-1.0, scalar2=None, op0=ALU.mult)
-        sort_x(1, 0)
-        sort_x(1, 1)
-        nc.vector.tensor_copy(out=c_all[:, : 2 * BANK].bitcast(F32), in_=c_banks[0][:])
-        nc.vector.tensor_copy(out=c_all[:, 2 * BANK :].bitcast(F32), in_=c_banks[1][:, : 2 * P])
 
         last = TILES - 1
-        for i in range(TILES):
+
+        def prepare(k):
+            mean_near(k)
+            quantise_a(k, 0)
+            invert_mean(k)
+            quantise_a(k, 1)
+
+        scores(0, 0)
+        sigmoid(0, 0)
+        spread_c()
+        scores(0, 1)
+        sort_x(1, 0)
+        sort_x(1, 1)
+        sigmoid(0, 1)
+        turn_x(1, 0)
+        turn_x(1, 1)
+        weigh(0, 0)
+        group_x(1, 0)
+        group_x(1, 1)
+        quantise_x(1, 0)
+        scores(0, 2)
+        weigh(0, 1)
+        quantise_x(1, 1)
+        sigmoid(0, 2)
+        sort_x(2, 0)
+        sort_x(2, 1)
+        weigh(0, 2)
+
+        for i in range(1, TILES):
+            k = 2 * (i - FIRST)
             scores(i, 0)
-            if i > LAG:
-                finish(i - LAG - 1)
-            if i > 0:
-                mean_near(i - 1)
-                some_v()
-                invert_mean(i - 1)
+            if i > FIRST:
+                finish(k - 1)
+            if i >= FIRST:
+                prepare(k)
+            some_v()
             sigmoid(i, 0)
             if i < last:
                 turn_x(i + 1, 0)
                 turn_x(i + 1, 1)
-            if i > 0:
-                turn_a(i - 1, 0)
-                turn_a(i - 1, 1)
+            turn_a(i - 1, 0)
+            turn_a(i - 1, 1)
             weigh(i, 0)
             if i < last:
                 group_x(i + 1, 0)
                 group_x(i + 1, 1)
                 quantise_x(i + 1, 0)
                 quantise_x(i + 1, 1)
-            if i == last:
-                profile(i - LAG, "o")
+            if i >= FIRST:
+                profile(k, "o")
+                prepare(k + 1)
             scores(i, 1)
-            if i > 0:
-                group_a(i - 1, 0)
-                group_a(i - 1, 1)
-            if i + 2 < TILES and i > 0:
+            group_a(i - 1, 0)
+            group_a(i - 1, 1)
+            if i + 2 < TILES:
                 sort_x(i + 2, 0)
                 sort_x(i + 2, 1)
-            if i > 0:
-                quantise_a(i - 1, 0)
-                quantise_a(i - 1, 1)
+            some_v()
+            if i >= FIRST:
+                finish(k)
             if i == last:
-                finish(i - LAG)
+                prepare(last - 1)
             sigmoid(i, 1)
             weigh(i, 1)
             if i == last:
-                profile(i - LAG + 1, "xt0")
+                profile(k + 1, "xt0")
             scores(i, 2)
-            some_v()
-            if i == 0:
-                some_v()
-                sort_x(2, 0)
-                sort_x(2, 1)
-            if i == 2:
-                some_v()
             if i == last:
-                finish(i - LAG + 1)
+                finish(k + 1)
             sigmoid(i, 2)
-            if LAG <= i < last:
-                profile(i - LAG, "o")
+            if FIRST <= i < last:
+                profile(k + 1, "o")
             if i < last:
                 weigh(i, 2)
 
@@ -332,4 +363,4 @@ def tile_msa_neighbour_reweighting_s9_kernel(tc, x, refs_words, refs_scales, the
         quantise_a(last, 1)
         finish(last - 1)
         profile(last, "o", range(2, NG))
-        finish(last)
+        finish(last, 2)

@@ -22,7 +22,7 @@ BANK = 512
 TILES = M // P
 KG = K // 512
 NG = N // 512
-FIRST = 5
+FIRST = 6
 
 
 def tile_msa_neighbour_reweighting_s9_kernel(tc, x, refs_words, refs_scales, theta, c, v, out):
@@ -39,6 +39,10 @@ def tile_msa_neighbour_reweighting_s9_kernel(tc, x, refs_words, refs_scales, the
         def bank(tag):
             return psum.tile([P, BANK], F32, name=tag, tag=tag)
 
+        c_cols = keep.tile([P, NG, 4], BF16)
+        nc.scalar.dma_start(out=c_cols[:], in_=c.rearrange("(g p t) -> p g t", p=P, t=4))
+        theta_sb = keep.tile([P, TILES], BF16)
+        nc.scalar.dma_start(out=theta_sb[:], in_=theta.rearrange("(p i) -> p i", i=TILES))
         x_half = {}
         for h in range(2):
             first = keep.tile([P, K // 2], BF16, name="x0_%d" % h)
@@ -84,20 +88,16 @@ def tile_msa_neighbour_reweighting_s9_kernel(tc, x, refs_words, refs_scales, the
                     at = g * width + (j - thirds[0]) * BANK
                     w_scales[j, g] = plane[:, at : at + BANK]
 
+        load_x(1)
         load_scales([0])
         load_w(0)
-        c_cols = keep.tile([P, NG, 4], BF16)
-        nc.scalar.dma_start(out=c_cols[:], in_=c.rearrange("(g p t) -> p g t", p=P, t=4))
-        theta_sb = keep.tile([P, TILES], BF16)
-        nc.scalar.dma_start(out=theta_sb[:], in_=theta.rearrange("(p i) -> p i", i=TILES))
         load_scales([1, 2])
         load_w(1)
-        load_x(1)
-        load_w(2)
         load_x(2)
+        load_w(2)
         load_v(0)
-        load_v(1)
         load_x(3)
+        load_v(1)
         load_v(2)
         for i in range(4, TILES):
             load_x(i)
@@ -143,7 +143,7 @@ def tile_msa_neighbour_reweighting_s9_kernel(tc, x, refs_words, refs_scales, the
             nc.vector.quantize_mx(out=x_codes[i][:, cols].bitcast(E4M3), scales=x_scales[i][:, cols], in_=x_grouped[i, h][:])
 
         def scores(i, j):
-            s_banks[i, j] = bank("s%d" % j)
+            s_banks[i, j] = bank("s%d" % (len(s_banks) % NG))
             for g in range(KG):
                 cols = slice(g * P, (g + 1) * P)
                 nc.tensor.matmul_mx(
@@ -169,7 +169,7 @@ def tile_msa_neighbour_reweighting_s9_kernel(tc, x, refs_words, refs_scales, the
             )
 
         def weigh(i, j):
-            a_rows[i, j] = work.tile([P, BANK], BF16, name="a_rows", bufs=6)
+            a_rows[i, j] = work.tile([P, BANK], BF16, name="a_rows", bufs=9)
             nc.vector.tensor_tensor(
                 out=a_rows[i, j][:], in0=near[i, j][:], in1=c_all[:, j * BANK : (j + 1) * BANK], op=ALU.mult
             )
@@ -185,8 +185,8 @@ def tile_msa_neighbour_reweighting_s9_kernel(tc, x, refs_words, refs_scales, the
             inv_mean[i] = keep.tile([P, 1], F32, name="inv_mean%d" % i)
             nc.vector.reciprocal(out=inv_mean[i][:], in_=mean[i][:])
 
-        def turn_a(i, b):
-            a_banks[i, b] = bank("at%d" % b)
+        def turn_a(i, b, tag="at"):
+            a_banks[i, b] = bank("%s%d" % (tag, b))
             for g in range(2 * b, min(2 * b + 2, NG)):
                 words = a_rows[i, g][:].bitcast(F32)
                 for u in range(2):
@@ -253,26 +253,28 @@ def tile_msa_neighbour_reweighting_s9_kernel(tc, x, refs_words, refs_scales, the
                 v_steps[0]()
                 v_steps.remove(v_steps[0])
 
-        for h in range(2):
-            sort_x(0, h)
-            turn_x(0, h)
-            group_x(0, h)
+        neg_theta = keep.tile([P, TILES], F32)
         c_all = keep.tile([P, N], BF16)
-        c_words = c_cols[:].rearrange("p g t -> p (g t)").bitcast(F32)
+        ident_bf = keep.tile([P, P], BF16)
+        c_banks = []
 
         def spread_c():
-            c_banks = [bank("at0"), bank("at1")]
-            for w in range(2 * NG):
-                nc.tensor.transpose(
-                    c_banks[w // 4][:, (w % 4) * P : (w % 4 + 1) * P], c_words[:, w : w + 1].to_broadcast([P, P]), ident[:]
-                )
-            nc.vector.tensor_copy(out=c_all[:, : 2 * BANK].bitcast(F32), in_=c_banks[0][:])
-            nc.vector.tensor_copy(out=c_all[:, 2 * BANK :].bitcast(F32), in_=c_banks[1][:, : 2 * P])
+            for g, tag in enumerate(["at0", "at1", "o"]):
+                c_banks.append(bank(tag))
+                for t in range(4):
+                    nc.tensor.matmul(
+                        c_banks[g][:, t * P : (t + 1) * P],
+                        lhsT=c_cols[:, g, t : t + 1].to_broadcast([P, P]),
+                        rhs=ident_bf[:],
+                        start=True,
+                        stop=True,
+                    )
 
-        quantise_x(0, 0)
-        quantise_x(0, 1)
-        neg_theta = keep.tile([P, TILES], F32)
-        nc.vector.tensor_scalar(out=neg_theta[:], in0=theta_sb[:], scalar1=-1.0, scalar2=None, op0=ALU.mult)
+        def keep_c(g):
+            nc.vector.tensor_copy(
+                out=c_all[:, g * BANK : (g + 1) * BANK].rearrange("m (u p e) -> m u p e", u=2, e=2),
+                in_=c_banks[g][:].rearrange("m (u e p) -> m u p e", u=2, e=2),
+            )
 
         last = TILES - 1
 
@@ -282,29 +284,47 @@ def tile_msa_neighbour_reweighting_s9_kernel(tc, x, refs_words, refs_scales, the
             invert_mean(k)
             quantise_a(k, 1)
 
-        scores(0, 0)
-        sigmoid(0, 0)
+        nc.vector.tensor_copy(out=ident_bf[:], in_=ident[:])
         spread_c()
-        scores(0, 1)
+        for h in range(2):
+            sort_x(0, h)
+            turn_x(0, h)
+            group_x(0, h)
+        nc.vector.tensor_scalar(out=neg_theta[:], in0=theta_sb[:], scalar1=-1.0, scalar2=None, op0=ALU.mult)
+        keep_c(0)
         sort_x(1, 0)
         sort_x(1, 1)
-        sigmoid(0, 1)
-        turn_x(1, 0)
-        turn_x(1, 1)
-        weigh(0, 0)
-        group_x(1, 0)
-        group_x(1, 1)
+        quantise_x(0, 0)
+        quantise_x(0, 1)
+        for h in range(2):
+            turn_x(1, h)
+            group_x(1, h)
+        keep_c(1)
+        keep_c(2)
         quantise_x(1, 0)
-        scores(0, 2)
-        weigh(0, 1)
         quantise_x(1, 1)
-        sigmoid(0, 2)
-        sort_x(2, 0)
-        sort_x(2, 1)
-        weigh(0, 2)
+        for j in range(NG):
+            if j == NG - 1:
+                turn_x(2, 0)
+                turn_x(2, 1)
+                group_x(2, 0)
+                group_x(2, 1)
+                quantise_x(2, 0)
+                quantise_x(2, 1)
+                sort_x(3, 0)
+                sort_x(3, 1)
+            for i in range(2):
+                scores(i, j)
+                sigmoid(i, j)
+                if (i, j) == (0, 1):
+                    sort_x(2, 0)
+                    sort_x(2, 1)
+                weigh(i, j)
 
-        for i in range(1, TILES):
-            k = 2 * (i - FIRST)
+        some_v()
+
+        for i in range(2, TILES):
+            k = 3 * (i - FIRST)
             scores(i, 0)
             if i > FIRST:
                 finish(k - 1)
@@ -315,8 +335,11 @@ def tile_msa_neighbour_reweighting_s9_kernel(tc, x, refs_words, refs_scales, the
             if i < last:
                 turn_x(i + 1, 0)
                 turn_x(i + 1, 1)
-            turn_a(i - 1, 0)
-            turn_a(i - 1, 1)
+            turn_a(i - 2, 0)
+            turn_a(i - 2, 1)
+            if i == last:
+                turn_a(i - 1, 0, "xt")
+                turn_a(i - 1, 1, "xt")
             weigh(i, 0)
             if i < last:
                 group_x(i + 1, 0)
@@ -327,26 +350,35 @@ def tile_msa_neighbour_reweighting_s9_kernel(tc, x, refs_words, refs_scales, the
                 profile(k, "o")
                 prepare(k + 1)
             scores(i, 1)
-            group_a(i - 1, 0)
-            group_a(i - 1, 1)
+            group_a(i - 2, 0)
+            if i >= FIRST:
+                finish(k)
+            group_a(i - 2, 1)
+            if i == last:
+                group_a(i - 1, 0)
             if i + 2 < TILES:
                 sort_x(i + 2, 0)
                 sort_x(i + 2, 1)
             some_v()
             if i >= FIRST:
-                finish(k)
-            if i == last:
-                prepare(last - 1)
+                prepare(k + 2)
             sigmoid(i, 1)
+            if i >= FIRST:
+                profile(k + 1, "o")
+            if i == last:
+                group_a(i - 1, 1)
+                profile(k + 2, "at1")
             weigh(i, 1)
             if i == last:
-                profile(k + 1, "xt0")
+                prepare(last - 1)
             scores(i, 2)
-            if i == last:
+            if i >= FIRST:
                 finish(k + 1)
+            if i == last:
+                finish(k + 2)
             sigmoid(i, 2)
             if FIRST <= i < last:
-                profile(k + 1, "o")
+                profile(k + 2, "o")
             if i < last:
                 weigh(i, 2)
 

@@ -39,32 +39,42 @@ def tile_msa_neighbour_reweighting_s9_kernel(tc, x, refs_words, refs_scales, the
         def bank(tag):
             return psum.tile([P, BANK], F32, name=tag, tag=tag)
 
+        blank = keep.tile([P, BANK], BF16)
+        nc.vector.memset(blank[:].bitcast(I32), 0)
+        warm_bank = bank("s2")
+
+        def warm_up(count):
+            for n in range(count):
+                nc.tensor.matmul(warm_bank[:], lhsT=blank[:, :P], rhs=blank[:], start=True, stop=True)
+
         c_cols = keep.tile([P, NG, 4], BF16)
         nc.scalar.dma_start(out=c_cols[:], in_=c.rearrange("(g p t) -> p g t", p=P, t=4))
         theta_sb = keep.tile([P, TILES], BF16)
         nc.scalar.dma_start(out=theta_sb[:], in_=theta.rearrange("(p i) -> p i", i=TILES))
         x_half = {}
-        for h in range(2):
-            first = keep.tile([P, K // 2], BF16, name="x0_%d" % h)
-            nc.sync.dma_start(out=first[:], in_=x_rows[:, 0, h * 1024 : (h + 1) * 1024])
-            x_half[0, h] = first[:]
 
-        def load_x(i):
-            whole = keep.tile([P, K], BF16, name="x%d" % i)
-            nc.sync.dma_start(out=whole[:], in_=x_rows[:, i, :])
-            for h in range(2):
-                x_half[i, h] = whole[:, h * 1024 : (h + 1) * 1024]
+        def load_x(i, pieces=1):
+            width = K // pieces
+            for piece in range(pieces):
+                part = keep.tile([P, width], BF16, name="x%d_%d" % (i, piece))
+                nc.sync.dma_start(out=part[:], in_=x_rows[:, i, piece * width : (piece + 1) * width])
+                for h in range(2 // pieces):
+                    x_half[i, piece + h] = part[:, h * K // 2 : (h + 1) * K // 2]
 
         ident = keep.tile([P, P], F32)
         make_identity(nc, ident[:])
 
-        w_codes = []
+        w_codes = {}
 
-        def load_w(j):
-            part = keep.tile([P, KG, 2 * BANK], U8, name="w%d" % j, align_bytes=64)
-            src = refs_words.rearrange("g p b -> p g b")[:, :, j * 2 * BANK : (j + 1) * 2 * BANK]
-            nc.sync.dma_start(out=part[:].bitcast(I32), in_=src.bitcast(I32))
-            w_codes.append(part)
+        def load_w(j, pieces):
+            groups = KG // pieces
+            for piece in range(pieces):
+                part = keep.tile([P, groups, 2 * BANK], U8, name="w%d_%d" % (j, piece), align_bytes=64)
+                first = piece * groups
+                src = refs_words.rearrange("g p b -> p g b")[:, first : first + groups, j * 2 * BANK : (j + 1) * 2 * BANK]
+                nc.sync.dma_start(out=part[:].bitcast(I32), in_=src.bitcast(I32))
+                for g in range(groups):
+                    w_codes[j, first + g] = part[:, g, :]
 
         v_raw = []
 
@@ -88,13 +98,14 @@ def tile_msa_neighbour_reweighting_s9_kernel(tc, x, refs_words, refs_scales, the
                     at = g * width + (j - thirds[0]) * BANK
                     w_scales[j, g] = plane[:, at : at + BANK]
 
+        load_x(0, 2)
         load_x(1)
         load_scales([0])
-        load_w(0)
+        load_w(0, 2)
         load_scales([1, 2])
-        load_w(1)
+        load_w(1, 2)
         load_x(2)
-        load_w(2)
+        load_w(2, 1)
         load_v(0)
         load_x(3)
         load_v(1)
@@ -150,7 +161,7 @@ def tile_msa_neighbour_reweighting_s9_kernel(tc, x, refs_words, refs_scales, the
                     out=s_banks[i, j][:],
                     lhsT=x_codes[i][:, cols].bitcast(E4M3),
                     lhsT_scale=x_scales[i][:, cols],
-                    rhs=w_codes[j][:, g, :].bitcast(E2M1),
+                    rhs=w_codes[j, g].bitcast(E2M1),
                     rhs_scale=w_scales[j, g],
                     start=(g == 0),
                     stop=(g == KG - 1),
@@ -285,12 +296,14 @@ def tile_msa_neighbour_reweighting_s9_kernel(tc, x, refs_words, refs_scales, the
             quantise_a(k, 1)
 
         nc.vector.tensor_copy(out=ident_bf[:], in_=ident[:])
+        warm_up(3)
         spread_c()
+        warm_up(0)
         for h in range(2):
             sort_x(0, h)
             turn_x(0, h)
             group_x(0, h)
-        nc.vector.tensor_scalar(out=neg_theta[:], in0=theta_sb[:], scalar1=-1.0, scalar2=None, op0=ALU.mult)
+        warm_up(2)
         keep_c(0)
         sort_x(1, 0)
         sort_x(1, 1)
@@ -299,10 +312,11 @@ def tile_msa_neighbour_reweighting_s9_kernel(tc, x, refs_words, refs_scales, the
         for h in range(2):
             turn_x(1, h)
             group_x(1, h)
-        keep_c(1)
-        keep_c(2)
+        nc.vector.tensor_scalar(out=neg_theta[:], in0=theta_sb[:], scalar1=-1.0, scalar2=None, op0=ALU.mult)
         quantise_x(1, 0)
         quantise_x(1, 1)
+        keep_c(1)
+        keep_c(2)
         for j in range(NG):
             if j == NG - 1:
                 turn_x(2, 0)
@@ -323,76 +337,81 @@ def tile_msa_neighbour_reweighting_s9_kernel(tc, x, refs_words, refs_scales, the
 
         some_v()
 
-        for i in range(2, TILES):
-            k = 3 * (i - FIRST)
+        for i in range(2, last):
+            second = i == last - 1
             scores(i, 0)
-            if i > FIRST:
-                finish(k - 1)
-            if i >= FIRST:
-                prepare(k)
             some_v()
+            if second:
+                prepare(0)
             sigmoid(i, 0)
-            if i < last:
-                turn_x(i + 1, 0)
-                turn_x(i + 1, 1)
+            turn_x(i + 1, 0)
+            turn_x(i + 1, 1)
             turn_a(i - 2, 0)
             turn_a(i - 2, 1)
-            if i == last:
-                turn_a(i - 1, 0, "xt")
-                turn_a(i - 1, 1, "xt")
             weigh(i, 0)
-            if i < last:
-                group_x(i + 1, 0)
-                group_x(i + 1, 1)
-                quantise_x(i + 1, 0)
-                quantise_x(i + 1, 1)
-            if i >= FIRST:
-                profile(k, "o")
-                prepare(k + 1)
+            group_x(i + 1, 0)
+            group_x(i + 1, 1)
+            quantise_x(i + 1, 0)
+            quantise_x(i + 1, 1)
             scores(i, 1)
             group_a(i - 2, 0)
-            if i >= FIRST:
-                finish(k)
             group_a(i - 2, 1)
-            if i == last:
-                group_a(i - 1, 0)
-            if i + 2 < TILES:
+            if second:
+                prepare(1)
+                profile(0, "o")
+            else:
                 sort_x(i + 2, 0)
                 sort_x(i + 2, 1)
-            some_v()
-            if i >= FIRST:
-                prepare(k + 2)
+                some_v()
             sigmoid(i, 1)
-            if i >= FIRST:
-                profile(k + 1, "o")
-            if i == last:
-                group_a(i - 1, 1)
-                profile(k + 2, "at1")
             weigh(i, 1)
-            if i == last:
-                prepare(last - 1)
             scores(i, 2)
-            if i >= FIRST:
-                finish(k + 1)
-            if i == last:
-                finish(k + 2)
+            if second:
+                finish(0)
+                prepare(2)
+                profile(1, "o")
             sigmoid(i, 2)
-            if FIRST <= i < last:
-                profile(k + 2, "o")
-            if i < last:
-                weigh(i, 2)
+            weigh(i, 2)
 
+        scores(last, 0)
+        finish(1)
+        prepare(3)
+        sigmoid(last, 0)
+        turn_a(last - 2, 0)
+        turn_a(last - 2, 1)
+        turn_a(last - 1, 0, "xt")
+        turn_a(last - 1, 1, "xt")
+        prepare(4)
+        weigh(last, 0)
+        profile(2, "o")
+        group_a(last - 2, 1)
+        group_a(last - 2, 0)
+        scores(last, 1)
+        finish(2)
+        group_a(last - 1, 0)
+        prepare(5)
+        sigmoid(last, 1)
+        profile(3, "o")
+        profile(4, "at1")
+        group_a(last - 1, 1)
+        weigh(last, 1)
+        prepare(6)
+        scores(last, 2)
+        finish(3)
+        finish(4)
+        sigmoid(last, 2)
         turn_a(last, 0)
         weigh(last, 2)
         group_a(last, 0)
-        profile(last - 1, "xt1")
+        profile(last - 2, "xt0")
         turn_a(last, 1)
         quantise_a(last, 0)
         mean_near(last)
+        finish(last - 2)
         group_a(last, 1)
-        profile(last, "o", range(2))
+        profile(last - 1, "xt1")
         invert_mean(last)
         quantise_a(last, 1)
         finish(last - 1)
-        profile(last, "o", range(2, NG))
+        profile(last, "o")
         finish(last, 2)

@@ -39,14 +39,6 @@ def tile_msa_neighbour_reweighting_s9_kernel(tc, x, refs_words, refs_scales, the
         def bank(tag):
             return psum.tile([P, BANK], F32, name=tag, tag=tag)
 
-        blank = keep.tile([P, BANK], BF16)
-        nc.vector.memset(blank[:].bitcast(I32), 0)
-        warm_bank = bank("s2")
-
-        def warm_up(count):
-            for n in range(count):
-                nc.tensor.matmul(warm_bank[:], lhsT=blank[:, :P], rhs=blank[:], start=True, stop=True)
-
         c_cols = keep.tile([P, NG, 4], BF16)
         nc.scalar.dma_start(out=c_cols[:], in_=c.rearrange("(g p t) -> p g t", p=P, t=4))
         theta_sb = keep.tile([P, TILES], BF16)
@@ -296,14 +288,11 @@ def tile_msa_neighbour_reweighting_s9_kernel(tc, x, refs_words, refs_scales, the
             quantise_a(k, 1)
 
         nc.vector.tensor_copy(out=ident_bf[:], in_=ident[:])
-        warm_up(3)
         spread_c()
-        warm_up(0)
         for h in range(2):
             sort_x(0, h)
             turn_x(0, h)
             group_x(0, h)
-        warm_up(2)
         keep_c(0)
         sort_x(1, 0)
         sort_x(1, 1)

from contextlib import ExitStack

import concourse.mybir as mybir
from concourse.masks import make_identity

M, K, N, D = 1024, 2048, 1536, 512
FLOPS = 2 * M * N * (K + D)

F32 = mybir.dt.float32
BF16 = mybir.dt.bfloat16
I32 = mybir.dt.int32
U32 = mybir.dt.uint32
U8 = mybir.dt.uint8
E4M3 = mybir.dt.float8_e4m3fn_x4
E5M2 = mybir.dt.float8_e5m2_x4
E2M1 = mybir.dt.float4_e2m1fn_x4
ACT = mybir.ActivationFunctionType
ALU = mybir.AluOpType

P = 128
BANK = 512
TILES = M // P
KG = K // 512
NG = N // 512
FIRST = 6


def tile_msa_neighbour_reweighting_s9_kernel(tc, x, refs_words, refs_scales, theta, c, v, out):
    nc = tc.nc
    x_rows = x.rearrange("(p i) k -> p i k", i=TILES)
    out_rows = out.rearrange("(p i) d -> p i d", i=TILES)

    with ExitStack() as ctx:
        keep = ctx.enter_context(tc.tile_pool(name="keep", bufs=1))
        work = ctx.enter_context(tc.tile_pool(name="work", bufs=3))
        psum = ctx.enter_context(tc.psum_pool(name="psum", bufs=1))
        ctx.enter_context(tc.manual_schedule())

        def bank(tag):
            return psum.tile([P, BANK], F32, name=tag, tag=tag)

        c_cols = keep.tile([P, NG, 4], BF16)
        nc.scalar.dma_start(out=c_cols[:], in_=c.rearrange("(g p t) -> p g t", p=P, t=4))
        theta_sb = keep.tile([P, TILES], BF16)
        nc.scalar.dma_start(out=theta_sb[:], in_=theta.rearrange("(p i) -> p i", i=TILES))
        x_half = {}

        def load_x(i, pieces=1):
            width = K // pieces
            for piece in range(pieces):
                part = keep.tile([P, width], BF16, name="x%d_%d" % (i, piece))
                nc.sync.dma_start(out=part[:], in_=x_rows[:, i, piece * width : (piece + 1) * width])
                for h in range(2 // pieces):
                    x_half[i, piece + h] = part[:, h * K // 2 : (h + 1) * K // 2]

        ident = keep.tile([P, P], F32)
        make_identity(nc, ident[:])

        w_codes = {}

        def load_w(j, pieces):
            groups = KG // pieces
            for piece in range(pieces):
                part = keep.tile([P, groups, 2 * BANK], U8, name="w%d_%d" % (j, piece), align_bytes=64)
                first = piece * groups
                src = refs_words.rearrange("g p b -> p g b")[:, first : first + groups, j * 2 * BANK : (j + 1) * 2 * BANK]
                nc.sync.dma_start(out=part[:].bitcast(I32), in_=src.bitcast(I32))
                for g in range(groups):
                    w_codes[j, first + g] = part[:, g, :]

        v_raw = []

        def load_v(g):
            rows = keep.tile([P, 4, D], BF16, name="v%d" % g)
            nc.sync.dma_start(out=rows[:], in_=v[g * 512 : (g + 1) * 512, :].rearrange("(p t) d -> p t d", t=4))
            v_raw.append(rows)

        w_scales = {}

        def load_scales(thirds):
            width = len(thirds) * BANK
            plane = keep.tile([P, KG * width], U8, name="w_scales%d" % thirds[0], align_bytes=64)
            nc.vector.memset(plane[:].bitcast(I32), 0)
            cols = slice(thirds[0] * BANK, thirds[0] * BANK + width)
            rows = refs_scales[:, :, cols].bitcast(I32).rearrange("g (q r) n -> r q g n", r=4)
            for r in range(4):
                nc.sync.dma_start(out=plane[r:P:32, :].bitcast(I32).rearrange("q (g n) -> q g n", g=KG), in_=rows[r])
            for j in thirds:
                for g in range(KG):
                    at = g * width + (j - thirds[0]) * BANK
                    w_scales[j, g] = plane[:, at : at + BANK]

        load_x(0, 2)
        load_x(1)
        load_scales([0])
        load_w(0, 2)
        load_scales([1, 2])
        load_w(1, 2)
        load_x(2)
        load_w(2, 1)
        load_v(0)
        load_x(3)
        load_v(1)
        load_v(2)
        for i in range(4, TILES):
            load_x(i)

        x_sorted, x_banks, x_grouped, x_codes, x_scales = {}, {}, {}, {}, {}
        s_banks, near, parts, a_rows = {}, {}, {}, {}
        a_banks, a_grouped, a_codes, a_scales = {}, {}, {}, {}
        mean, inv_mean, o_banks = {}, {}, {}

        def sort_x(i, h):
            x_sorted[i, h] = work.tile([P, BANK], F32, name="x_sorted", bufs=4)
            nc.vector.tensor_copy(
                out=x_sorted[i, h][:].rearrange("m (u a w) -> m a u w", u=2, w=4),
                in_=x_half[i, h].bitcast(F32).rearrange("m (a w u) -> m a u w", u=2, w=4),
            )

        def turn_x(i, h):
            x_banks[i, h] = bank("xt%d" % h)
            for g in range(2):
                for u in range(2):
                    nc.tensor.transpose(
                        x_banks[i, h][:, (2 * g + u) * P : (2 * g + u + 1) * P],
                        x_sorted[i, h][:, (2 * u + g) * P : (2 * u + g + 1) * P],
                        ident[:],
                    )

        def group_words(src_bank, groups, name, bufs):
            grouped = work.tile([P, groups * BANK], BF16, name=name, align_bytes=64, bufs=bufs)
            nc.scalar.copy(
                out=grouped[:].bitcast(F32).rearrange("p (g m u) -> p g m u", u=2, m=P),
                in_=src_bank[:, : groups * 2 * P].rearrange("p (g u m) -> p g m u", u=2, m=P),
            )
            return grouped

        def group_x(i, h):
            x_grouped[i, h] = group_words(x_banks[i, h], 2, "x_grouped", 3)

        def quantise_x(i, h):
            if h == 0:
                x_codes[i] = work.tile([P, KG * P], U32, name="x_codes", align_bytes=64)
                x_scales[i] = work.tile([P, KG * P], U8, name="x_scales", align_bytes=64)
            cols = slice(h * 2 * P, (h + 1) * 2 * P)
            nc.vector.quantize_mx(out=x_codes[i][:, cols].bitcast(E4M3), scales=x_scales[i][:, cols], in_=x_grouped[i, h][:])

        def scores(i, j):
            s_banks[i, j] = bank("s%d" % (len(s_banks) % NG))
            for g in range(KG):
                cols = slice(g * P, (g + 1) * P)
                nc.tensor.matmul_mx(
                    out=s_banks[i, j][:],
                    lhsT=x_codes[i][:, cols].bitcast(E4M3),
                    lhsT_scale=x_scales[i][:, cols],
                    rhs=w_codes[j, g].bitcast(E2M1),
                    rhs_scale=w_scales[j, g],
                    start=(g == 0),
                    stop=(g == KG - 1),
                )

        def sigmoid(i, j):
            if j == 0:
                parts[i] = keep.tile([P, NG], F32, name="parts%d" % i)
            near[i, j] = work.tile([P, BANK], F32, name="near")
            nc.scalar.activation(
                out=near[i, j][:].rearrange("m (u p e) -> m u p e", u=2, e=2),
                in_=s_banks[i, j][:].rearrange("m (p u e) -> m u p e", u=2, e=2),
                func=ACT.Sigmoid,
                bias=neg_theta[:, i : i + 1],
                accum_out=parts[i][:, j : j + 1],
            )

        def weigh(i, j):
            a_rows[i, j] = work.tile([P, BANK], BF16, name="a_rows", bufs=9)
            nc.vector.tensor_tensor(
                out=a_rows[i, j][:], in0=near[i, j][:], in1=c_all[:, j * BANK : (j + 1) * BANK], op=ALU.mult
            )

        def mean_near(i):
            shares = work.tile([P, NG], F32, name="shares")
            mean[i] = work.tile([P, 1], F32, name="mean")
            nc.vector.tensor_scalar(
                out=shares[:], in0=parts[i][:], scalar1=1.0 / N, scalar2=None, op0=ALU.mult, op1=ALU.add, accum_out=mean[i][:]
            )

        def invert_mean(i):
            inv_mean[i] = keep.tile([P, 1], F32, name="inv_mean%d" % i)
            nc.vector.reciprocal(out=inv_mean[i][:], in_=mean[i][:])

        def turn_a(i, b, tag="at"):
            a_banks[i, b] = bank("%s%d" % (tag, b))
            for g in range(2 * b, min(2 * b + 2, NG)):
                words = a_rows[i, g][:].bitcast(F32)
                for u in range(2):
                    at = (2 * (g - 2 * b) + u) * P
                    nc.tensor.transpose(a_banks[i, b][:, at : at + P], words[:, u * P : (u + 1) * P], ident[:])

        def group_a(i, b):
            a_grouped[i, b] = group_words(a_banks[i, b], 2 - b, "a_grouped%d" % b, FIRST + 1)

        def quantise_a(i, b):
            if b == 0:
                a_codes[i] = keep.tile([P, NG * P], U32, name="a_codes%d" % i, align_bytes=64)
                a_scales[i] = keep.tile([P, NG * P], U8, name="a_scales%d" % i, align_bytes=64)
            cols = slice(b * 2 * P, min((b + 1) * 2 * P, NG * P))
            nc.vector.quantize_mx(out=a_codes[i][:, cols].bitcast(E5M2), scales=a_scales[i][:, cols], in_=a_grouped[i, b][:])

        def profile(i, tag, groups=range(NG)):
            if 0 in groups:
                o_banks[i] = bank(tag)
            for g in groups:
                cols = slice(g * P, (g + 1) * P)
                nc.tensor.matmul_mx(
                    out=o_banks[i][:],
                    lhsT=a_codes[i][:, cols].bitcast(E5M2),
                    lhsT_scale=a_scales[i][:, cols],
                    rhs=v_codes[:, g * D : (g + 1) * D].bitcast(E4M3),
                    rhs_scale=v_scales[:, g * D : (g + 1) * D],
                    start=(g == 0),
                    stop=(g == NG - 1),
                )

        def finish(i, pieces=1):
            result = work.tile([P, D], F32, name="result")
            for piece in range(pieces):
                cols = slice(piece * D // pieces, (piece + 1) * D // pieces)
                nc.scalar.activation(out=result[:, cols], in_=o_banks[i][:, cols], func=ACT.Copy, scale=inv_mean[i][:])
                nc.sync.dma_start(out=out_rows[:, i, cols], in_=result[:, cols])

        v_grouped = {}
        v_codes = keep.tile([P, NG * D], U32, align_bytes=64)
        v_scales = keep.tile([P, NG * D], U8, align_bytes=64)

        def group_v(g, h):
            if h == 0:
                v_grouped[g] = keep.tile([P, D, 4], BF16, name="v_grouped%d" % g, align_bytes=64)
            cols = slice(h * D // 2, (h + 1) * D // 2)
            nc.vector.tensor_copy(
                out=v_grouped[g][:, cols, :].rearrange("p (a w) t -> p a t w", w=4),
                in_=v_raw[g][:, :, cols].rearrange("p t (a w) -> p a t w", w=4),
            )

        def quantise_v(g):
            cols = slice(g * D, (g + 1) * D)
            nc.vector.quantize_mx(
                out=v_codes[:, cols].bitcast(E4M3), scales=v_scales[:, cols], in_=v_grouped[g][:].rearrange("p d t -> p (d t)")
            )

        v_steps = []
        for g in range(NG):
            v_steps.extend([lambda g=g: group_v(g, 0), lambda g=g: group_v(g, 1), lambda g=g: quantise_v(g)])

        def some_v():
            if v_steps:
                v_steps[0]()
                v_steps.remove(v_steps[0])

        neg_theta = keep.tile([P, TILES], F32)
        c_all = keep.tile([P, N], BF16)
        ident_bf = keep.tile([P, P], BF16)
        c_banks = []

        def spread_c():
            for g, tag in enumerate(["at0", "at1", "o"]):
                c_banks.append(bank(tag))
                for t in range(4):
                    nc.tensor.matmul(
                        c_banks[g][:, t * P : (t + 1) * P],
                        lhsT=c_cols[:, g, t : t + 1].to_broadcast([P, P]),
                        rhs=ident_bf[:],
                        start=True,
                        stop=True,
                    )

        def keep_c(g):
            nc.vector.tensor_copy(
                out=c_all[:, g * BANK : (g + 1) * BANK].rearrange("m (u p e) -> m u p e", u=2, e=2),
                in_=c_banks[g][:].rearrange("m (u e p) -> m u p e", u=2, e=2),
            )

        last = TILES - 1

        def prepare(k):
            mean_near(k)
            quantise_a(k, 0)
            invert_mean(k)
            quantise_a(k, 1)

        nc.vector.tensor_copy(out=ident_bf[:], in_=ident[:])
        spread_c()
        for h in range(2):
            sort_x(0, h)
            turn_x(0, h)
            group_x(0, h)
        keep_c(0)
        sort_x(1, 0)
        sort_x(1, 1)
        quantise_x(0, 0)
        quantise_x(0, 1)
        for h in range(2):
            turn_x(1, h)
            group_x(1, h)
        nc.vector.tensor_scalar(out=neg_theta[:], in0=theta_sb[:], scalar1=-1.0, scalar2=None, op0=ALU.mult)
        quantise_x(1, 0)
        quantise_x(1, 1)
        keep_c(1)
        keep_c(2)
        for j in range(NG):
            if j == NG - 1:
                turn_x(2, 0)
                turn_x(2, 1)
                group_x(2, 0)
                group_x(2, 1)
                quantise_x(2, 0)
                quantise_x(2, 1)
                sort_x(3, 0)
                sort_x(3, 1)
            for i in range(2):
                scores(i, j)
                sigmoid(i, j)
                if (i, j) == (0, 1):
                    sort_x(2, 0)
                    sort_x(2, 1)
                weigh(i, j)

        some_v()

        for i in range(2, last):
            second = i == last - 1
            scores(i, 0)
            some_v()
            if second:
                prepare(0)
            sigmoid(i, 0)
            turn_x(i + 1, 0)
            turn_x(i + 1, 1)
            turn_a(i - 2, 0)
            turn_a(i - 2, 1)
            weigh(i, 0)
            group_x(i + 1, 0)
            group_x(i + 1, 1)
            quantise_x(i + 1, 0)
            quantise_x(i + 1, 1)
            scores(i, 1)
            group_a(i - 2, 0)
            group_a(i - 2, 1)
            if second:
                prepare(1)
                profile(0, "o")
            else:
                sort_x(i + 2, 0)
                sort_x(i + 2, 1)
                some_v()
            sigmoid(i, 1)
            weigh(i, 1)
            scores(i, 2)
            if second:
                finish(0)
                prepare(2)
                profile(1, "o")
            sigmoid(i, 2)
            weigh(i, 2)

        scores(last, 0)
        finish(1)
        prepare(3)
        sigmoid(last, 0)
        turn_a(last - 2, 0)
        turn_a(last - 2, 1)
        turn_a(last - 1, 0, "xt")
        turn_a(last - 1, 1, "xt")
        prepare(4)
        weigh(last, 0)
        profile(2, "o")
        group_a(last - 2, 1)
        group_a(last - 2, 0)
        scores(last, 1)
        finish(2)
        group_a(last - 1, 0)
        prepare(5)
        sigmoid(last, 1)
        profile(3, "o")
        profile(4, "at1")
        group_a(last - 1, 1)
        weigh(last, 1)
        prepare(6)
        scores(last, 2)
        finish(3)
        finish(4)
        sigmoid(last, 2)
        turn_a(last, 0)
        weigh(last, 2)
        group_a(last, 0)
        profile(last - 2, "xt0")
        turn_a(last, 1)
        quantise_a(last, 0)
        mean_near(last)
        finish(last - 2)
        group_a(last, 1)
        profile(last - 1, "xt1")
        invert_mean(last)
        quantise_a(last, 1)
        finish(last - 1)
        profile(last, "o")
        finish(last, 2)
